import numpy as np
import ml_dtypes


def mxq(x, axis, fmt="e4m3"):
    dtype, down = {"e4m3": (ml_dtypes.float8_e4m3fn, 7), "e5m2": (ml_dtypes.float8_e5m2, 14)}[fmt]
    v = np.moveaxis(np.asarray(x, np.float32).astype(ml_dtypes.bfloat16).astype(np.float64), axis, -1)
    blocks = v.reshape(v.shape[:-1] + (-1, 32))
    amax = np.abs(blocks).max(-1, keepdims=True)
    byte = np.maximum(np.where(amax > 0, np.frexp(amax)[1] - 1 + 127, 0) - down, 1)
    scale = np.exp2(byte - 127.0)
    codes = (blocks / scale).astype(np.float32).astype(dtype).astype(np.float64)
    return np.moveaxis((codes * scale).reshape(v.shape), -1, axis)


WIDE = False


def mx_kscale(k):
    if not WIDE:
        return np.ones(k)
    levels = np.array([10, -10, 5, -5, 0])
    if k % 512:
        return np.exp2(np.random.permutation(np.resize(levels, k // 32))).repeat(32)
    a = np.empty((k // 512, 16))
    for p in range(k // 512):
        a[p, :8] = np.random.permutation(np.resize(levels, 8))
        for g in range(8):
            far = levels[np.abs(levels - a[p, g]) >= 10]
            a[p, g + 8] = far[np.random.randint(len(far))]
    return np.exp2(a.ravel()).repeat(32)


BF16 = ml_dtypes.bfloat16


def bf(x):
    return np.asarray(x, np.float32).astype(BF16)


def f64(x):
    return np.asarray(x).astype(np.float64)


E2M1 = np.array([0.0, 0.5, 1.0, 1.5, 2.0, 3.0, 4.0, 6.0, -0.0, -0.5, -1.0, -1.5, -2.0, -3.0, -4.0, -6.0])


def pack_weight(w, fmt):
    k, n = w.shape
    w = f64(bf(w)).reshape(k // 32, 32, n)
    amax = np.abs(w).max(1)
    if fmt == "e4m3":
        byte = np.frexp(amax)[1] - 1 + 127 - 7
    else:
        mant, ex = np.frexp(amax / 6.0)
        byte = np.where(mant > 0.5, ex, ex - 1) + 127
    byte = np.clip(np.where(amax > 0, byte, 1), 1, 254)
    scaled = (w * np.exp2(127.0 - byte)[:, None, :]).reshape(k, n).astype(np.float32)
    by_word = np.ascontiguousarray(scaled.reshape(k // 512, 128, 4, n).transpose(0, 1, 3, 2))
    if fmt == "e4m3":
        words = by_word.astype(ml_dtypes.float8_e4m3fn).view(np.uint8)
    else:
        c = by_word.astype(ml_dtypes.float4_e2m1fn).view(np.uint8) & 0xF
        words = c[..., 0::2] | (c[..., 1::2] << 4)
    return np.ascontiguousarray(words), np.ascontiguousarray(byte.astype(np.uint8).reshape(k // 512, 16, n))


def unpack_weight(words, scales, fmt):
    g, p, n, _ = words.shape
    if fmt == "e4m3":
        vals = np.ascontiguousarray(words).view(ml_dtypes.float8_e4m3fn).astype(np.float64)
    else:
        nib = np.empty((g, p, n, 4), np.uint8)
        nib[..., 0::2] = words & 0xF
        nib[..., 1::2] = words >> 4
        vals = E2M1[nib]
    vals = vals * np.repeat(np.exp2(scales.astype(np.float64) - 127.0), 8, axis=1)[..., None]
    return vals.transpose(0, 1, 3, 2).reshape(g * 512, n)
def pack4(w):
    words, scales = pack_weight(w, "e2m1")
    return words.reshape(words.shape[0], 128, -1), scales


def unpack4(words, scales):
    return unpack_weight(words.reshape(words.shape[0], 128, -1, 2), scales, "e2m1")


def planes(Y):
    n, m = Y.shape
    b = f64(bf(Y)).reshape(n // 32, 32, m)
    amax = np.abs(b).max(1)
    byte = np.clip(np.where(amax > 0, np.frexp(amax)[1] - 1 + 127 - 7, 1), 1, 254)
    codes = (b * np.exp2(127.0 - byte)[:, None, :]).reshape(n, m).astype(np.float32).astype(ml_dtypes.float8_e4m3fn).view(np.uint8)
    words = codes.reshape(n // 512, 128, 4, m).transpose(0, 1, 3, 2)
    return np.ascontiguousarray(words), np.ascontiguousarray(byte.astype(np.uint8).reshape(n // 512, 16, m))


N, D, C = 1024, 512, 1536
SPREAD = 1.5

def setup_inputs():
    rn = np.random.randn
    s, v, t = mx_kscale(D), mx_kscale(N), mx_kscale(N)
    q2 = SPREAD * rn(N, D) / np.sqrt(D)
    k2_words, k2_scales = pack4(rn(D, N) / s[:, None])
    m1 = np.exp(SPREAD * rn(N, N) + 0.3 * rn(N, 1) - SPREAD ** 2 / 2) / N + np.eye(N)
    w1 = 1.0 / m1.sum(axis=1)
    m1t_words, m1t_scales = pack_weight(np.ascontiguousarray((m1 * v[None, :]).T), "e4m3")
    r0 = np.exp(0.8 * rn(N, C) + 0.5 * rn(1, C))
    u = np.exp(0.3 * rn(N) - SPREAD ** 2 / 2) / N
    token = np.exp(0.8 * rn(N))
    return {"q2": bf(q2 * s[None, :]), "k2_words": k2_words, "k2_scales": k2_scales,
            "m1t_words": m1t_words, "m1t_scales": m1t_scales, "r0": bf(r0 / v[:, None]),
            "u": bf(u * t), "w1": bf(w1 / t), "w2": bf(0.5 * token), "b2": bf(0.5 * token * t)}

def reference(q2, k2_words, k2_scales, m1t_words, m1t_scales, r0, u, w1, w2, b2):
    K2 = unpack4(k2_words, k2_scales)
    M1T = unpack_weight(m1t_words, m1t_scales, "e4m3")
    S2 = mxq(f64(q2), 1, "e4m3") @ K2
    E2 = np.exp(S2) * f64(u)[None, :]
    R1 = (M1T.T @ mxq(f64(r0), 0, "e4m3")) * f64(w1)[:, None]
    Z = mxq(E2, 1, "e4m3") @ mxq(R1, 0, "e4m3")
    y = f64(w2)[:, None] * Z + f64(b2)[:, None] * R1
    Y = y.reshape(N, C)
    words, scales = planes(Y)
    return y, words, scales

@@ -1,0 +1,269 @@
+from contextlib import ExitStack
+
+import concourse.mybir as mybir
+from concourse.masks import make_identity
+
+N, D, C = 1024, 512, 1536
+FLOPS = 2 * N * N * D + 2 * 2 * N * N * C
+
+F32 = mybir.dt.float32
+BF16 = mybir.dt.bfloat16
+I32 = mybir.dt.int32
+U32 = mybir.dt.uint32
+U8 = mybir.dt.uint8
+FP8X4 = mybir.dt.float8_e4m3fn_x4
+FP4X4 = mybir.dt.float4_e2m1fn_x4
+ALU = mybir.AluOpType
+ACT = mybir.ActivationFunctionType
+
+P = 128
+T = 4
+G = N // (P * T)
+W = 512
+CHUNKS = [512, 512, 512]
+STARTS = [sum(CHUNKS[:c]) for c in range(len(CHUNKS))]
+
+ORDER = [
+    ("setup",), ("lv", "u"), ("lq", 1), ("log",), ("sumlog",), ("lms",),
+    ("lr", 1, 0), ("tq", 1), ("eq", 1, "a"), ("lq", 0), ("tq", 0), ("il", "r0", 1, 0, "v"),
+    ("lks",), ("lk",), ("psc",), ("qz", "q", 1, 0), ("eq", 0, "a"), ("pk2", 0),
+    ("pk2", 1), ("lr", 1, 2), ("qz", "q", 0, 0), ("lr", 1, 1), ("qz", "r0", 1, 0), ("il", "r0", 1, 1, "v"),
+    ("lm", 0), ("lv", "b2"), ("il", "r0", 1, 2, "a"), ("qz", "r0", 1, 2), ("lr", 0, 2), ("il", "r0", 0, 2, "v"),
+    ("qz", "r0", 1, 1), ("mm", "e", 0, 1), ("ev", "e", 0, 1, "a"), ("mm", "e", 1, 1), ("qz", "r0", 0, 2), ("ev", "e", 1, 1, "a"),
+    ("lr", 0, 1), ("lr", 0, 0), ("mm", "e", 0, 0), ("il", "e", 0, 1, "va"), ("mm", "e", 1, 0), ("il", "r0", 0, 0, "v"),
+    ("lm", 1), ("pm1", 1), ("lv", "w2"), ("pm1", 0), ("ev", "e", 0, 0, "a"), ("qz", "e", 0, 1),
+    ("ev", "e", 1, 0, "a"), ("lv", "w1"), ("qz", "r0", 0, 0), ("mm", "r1", 1, 0), ("signs",), ("il", "e", 1, 1, "v"),
+    ("il", "r0", 0, 1, "va"), ("qz", "e", 1, 1), ("il", "e", 0, 0, "v"), ("ev", "r1", 1, 0, "a"), ("il", "e", 1, 0, "v"), ("res", 1, 0, "v"),
+    ("mm", "r1", 0, 0), ("qz", "r0", 0, 1), ("mm", "r1", 0, 1), ("ev", "r1", 0, 0, "a"), ("il", "r1", 1, 0, "va"), ("qz", "e", 1, 0),
+    ("res", 0, 0, "v"), ("ev", "r1", 0, 1, "a"), ("mm", "r1", 1, 1), ("ev", "r1", 1, 1, "a"), ("il", "r1", 0, 0, "v"), ("res", 0, 1, "v"),
+    ("qz", "r1", 1, 0), ("mm", "r1", 0, 2), ("ev", "r1", 0, 2, "a"), ("qz", "e", 0, 0), ("qz", "r1", 0, 0), ("mm", "y", 0, 0),
+    ("il", "r1", 1, 1, "v"), ("ev", "y", 0, 0, "v"), ("qz", "r1", 1, 1), ("il", "r1", 0, 1, "a"), ("il", "y", 0, 0, "v"), ("mm", "y", 1, 0),
+    ("qz", "r1", 0, 1), ("qz", "y", 0, 0), ("mm", "r1", 1, 2), ("il", "r1", 0, 2, "a"), ("ev", "y", 1, 0, "v"), ("qz", "r1", 0, 2),
+    ("ev", "r1", 1, 2, "a"), ("res", 1, 1, "a"), ("il", "r1", 1, 2, "a"), ("sy", 0, 0), ("res", 0, 2, "a"), ("sy", 1, 0),
+    ("mm", "y", 1, 1), ("ev", "y", 1, 1, "v"), ("sw", 0, 0), ("mm", "y", 0, 1), ("ev", "y", 0, 1, "v"), ("qz", "r1", 1, 2),
+    ("mm", "y", 0, 2), ("res", 1, 2, "v"), ("mm", "y", 1, 2), ("sy", 1, 1), ("sy", 0, 1), ("ev", "y", 0, 2, "v"),
+    ("sy", 0, 2), ("ev", "y", 1, 2, "v"), ("il", "y", 0, 1, "va"), ("il", "y", 1, 0, "a"), ("il", "y", 0, 2, "a"), ("sy", 1, 2),
+    ("qz", "y", 0, 2), ("qz", "y", 0, 1), ("qz", "y", 1, 0), ("ss", 0, "s"), ("sw", 0, 2), ("il", "y", 1, 1, "a"),
+    ("sw", 0, 1), ("il", "y", 1, 2, "va"), ("qz", "y", 1, 1), ("sw", 1, 0), ("sw", 1, 1), ("qz", "y", 1, 2),
+    ("ss", 1, "a"), ("sw", 1, 2),
+]
+
+
+def tile_rollout_two_layers_k4_kernel(tc, q2, k2_words, k2_scales, m1t_words, m1t_scales, r0, u, w1, w2, b2, out_0, out_1, out_2):
+    nc = tc.nc
+    with ExitStack() as ctx:
+        keep = ctx.enter_context(tc.tile_pool(name="keep", bufs=1))
+        stage = ctx.enter_context(tc.tile_pool(name="stage", bufs=2))
+        psum = ctx.enter_context(tc.psum_pool(name="psum", bufs=8))
+        ctx.enter_context(tc.manual_schedule())
+
+        def kept(name, shape, dtype):
+            return keep.tile(shape, dtype, name=name, align_bytes=64)
+
+        vec = {}
+        for name in ("u", "w1", "w2", "b2"):
+            vec[name] = kept("vec_" + name, [P, G * T], BF16)
+        ident = kept("ident", [P, P], F32)
+        sc_raw = kept("sc_raw", [P, N], U8)
+        sc = kept("sc", [P, N], U8)
+        k2_raw = kept("k2_raw", [P, 2 * N], U8)
+        k2 = kept("k2", [P, 2 * N], U8)
+        m1_raw = kept("m1_raw", [P, G, N], I32)
+        m1 = kept("m1", [P, G, N], I32)
+        q_raw = kept("q_raw", [P, G, T, D], BF16)
+        r0_raw = {}
+        acc = {}
+        for g in range(G):
+            for c, width in enumerate(CHUNKS):
+                r0_raw[g, c] = kept("r0_raw%d_%d" % (g, c), [P, T, width], BF16)
+                acc[g, c] = kept("acc%d_%d" % (g, c), [P, T, width], F32)
+        codes = {}
+        planes = {}
+        for name, cols in (("q", [G, W]), ("r0", [G, C]), ("e", [G, N]), ("r1", [G, C]), ("y", [G, C])):
+            codes[name] = kept("codes_" + name, [P] + cols, U32)
+            planes[name] = kept("plane_" + name, [P] + cols, U8)
+        mag = kept("mag", [P, G * T], F32)
+        parts = kept("parts", [P, 4, G * T], F32)
+        logs = kept("logs", [P, 4, G * T], F32)
+        log_u = kept("log_u", [P, G * T], F32)
+        sign2 = kept("sign2", [P, G * T], F32)
+        w1s = kept("w1s", [P, G * T], F32)
+        b2s = kept("b2s", [P, G * T], F32)
+        warm = kept("warm", [P, 2], F32)
+        banks = {}
+        rows = {}
+        packed = {}
+
+        def cols(c, kind="r0"):
+            if kind in ("q", "e"):
+                return slice(c * W, (c + 1) * W)
+            return slice(STARTS[c], STARTS[c] + CHUNKS[c])
+
+        def width(kind, c):
+            return W if kind in ("q", "e") else CHUNKS[c]
+
+        def load_vec(name, src, queue):
+            queue.dma_start(out=vec[name][:].rearrange("p (g t) -> p g t", t=T), in_=src.rearrange("(g p t) -> p g t", g=G, t=T))
+
+        def load_r0(g, c):
+            nc.sync.dma_start(out=r0_raw[g, c][:], in_=r0[g * 512:(g + 1) * 512, cols(c)].rearrange("(p t) w -> p t w", t=T))
+
+        def load_q(h):
+            nc.sync.dma_start(out=q_raw[:, h], in_=q2[h * 512:(h + 1) * 512, :].rearrange("(m t) d -> m t d", t=T))
+
+        def load_m1(k):
+            nc.sync.dma_start(out=m1_raw[:, k], in_=m1t_words[k].rearrange("p n t -> p (n t)").bitcast(I32))
+
+        def setup():
+            nc.vector.memset(sc_raw[:].bitcast(I32), 0)
+            make_identity(nc, ident[:])
+
+        def load_small(name):
+            load_vec(name, {"u": u, "w1": w1, "w2": w2, "b2": b2}[name], nc.sync if name == "u" else nc.gpsimd)
+
+        def load_k2():
+            nc.sync.dma_start(out=k2_raw[:].bitcast(I32), in_=k2_words[0].bitcast(I32))
+
+        def load_k2_scales():
+            for q in range(4):
+                nc.sync.dma_start(out=sc_raw[32 * q:32 * q + 4, :].bitcast(I32), in_=k2_scales[0, 4 * q:4 * q + 4, :].bitcast(I32))
+
+        def load_m1_scales():
+            for q in range(4):
+                nc.sync.dma_start(out=sc_raw[32 * q + 4:32 * q + 12, :].bitcast(I32), in_=m1t_scales[:, 4 * q:4 * q + 4, :].bitcast(I32))
+
+        def log_of_u():
+            nc.vector.scalar_tensor_tensor(out=mag[:], in0=vec["u"][:], scalar=-1.0, in1=vec["u"][:], op0=ALU.mult, op1=ALU.max)
+            nc.vector.tensor_scalar(out=sign2[:], in0=vec["u"][:], scalar1=0.0, scalar2=2.0, op0=ALU.is_ge, op1=ALU.mult)
+            nc.vector.tensor_scalar(out=parts[:, 0], in0=mag[:], scalar1=2.0 ** -63, scalar2=2.0 ** 64, op0=ALU.max, op1=ALU.min)
+            nc.vector.tensor_scalar(out=parts[:, 1], in0=mag[:], scalar1=2.0 ** 64, scalar2=2.0 ** -64, op0=ALU.max, op1=ALU.mult)
+            nc.vector.tensor_scalar(out=parts[:, 2], in0=mag[:], scalar1=2.0 ** -126, scalar2=2.0 ** -63, op0=ALU.max, op1=ALU.min)
+            nc.vector.tensor_scalar(out=logs[:, 3], in0=mag[:], scalar1=2.0 ** -126, scalar2=-(2.0 ** 100), op0=ALU.is_lt, op1=ALU.mult)
+            nc.scalar.activation(out=logs[:, 0:2], in_=parts[:, 0:2], func=ACT.Ln)
+            nc.scalar.activation(out=logs[:, 2], in_=parts[:, 2], func=ACT.Ln, scale=2.0 ** 63)
+            nc.scalar.activation(out=warm[:, 0:1], in_=logs[:, 2, 0:1], func=ACT.Exp)
+
+        def sum_logs():
+            nc.vector.tensor_reduce(out=log_u[:], in_=logs[:].rearrange("p k j -> p j k"), axis=mybir.AxisListType.X, op=ALU.add)
+
+        def signed_scales():
+            nc.vector.scalar_tensor_tensor(out=w1s[:], in0=sign2[:], scalar=1.0, in1=vec["w1"][:], op0=ALU.subtract, op1=ALU.mult)
+            nc.vector.scalar_tensor_tensor(out=b2s[:], in0=sign2[:], scalar=1.0, in1=vec["b2"][:], op0=ALU.subtract, op1=ALU.mult)
+
+        def permute_k2(g):
+            s = slice(g * 1024, (g + 1) * 1024)
+            nc.vector.tensor_copy(out=k2[:, s].rearrange("p (t m b) -> p t m b", t=T, b=2), in_=k2_raw[:, s].rearrange("p (m t b) -> p t m b", t=T, b=2))
+
+        def permute_scales():
+            nc.vector.tensor_copy(out=sc[:].rearrange("p (g t m) -> p g t m", g=G, t=T), in_=sc_raw[:].rearrange("p (g m t) -> p g t m", g=G, t=T))
+
+        def permute_m1(k):
+            nc.vector.tensor_copy(out=m1[:, k].rearrange("p (g t m) -> p g t m", g=G, t=T), in_=m1_raw[:, k].rearrange("p (g m t) -> p g t m", g=G, t=T))
+
+        def transpose_q(h):
+            words = q_raw[:, h].bitcast(F32)
+            for half in range(2):
+                bank = psum.tile([P, 2, 2, P], F32, tag="bank", name="bank")
+                banks["q", h, half] = bank
+                for s in range(2):
+                    for e in range(2):
+                        nc.tensor.transpose(bank[:, s, e, :], words[:, 2 * half + s, e:256:2], ident[:])
+
+        def evac_q(h, engine):
+            dst = stage.tile([P, W, T], BF16, tag="packed", name="packed", bufs=4, align_bytes=64)
+            packed["q", h, 0] = dst
+            words = dst[:].rearrange("p w t -> p (w t)").bitcast(F32)
+            for half in range(2):
+                copy = nc.scalar.copy if engine == "a" else nc.vector.tensor_copy
+                copy(out=words[:, half * 512:(half + 1) * 512].rearrange("p (s m e) -> p s m e", s=2, e=2), in_=banks["q", h, half][:].rearrange("p s e m -> p s m e"))
+
+        def matmuls(kind, a, b):
+            for t in range(T):
+                whole = psum.tile([P, W], F32, tag="bank", name="bank")
+                bank = whole[:, 0:width(kind, b)]
+                banks[kind, a, b, t] = bank
+                if kind == "e":
+                    j = slice(a * 512 + t * P, a * 512 + (t + 1) * P)
+                    nc.tensor.matmul_mx(out=bank[:], lhsT=k2[:, 2 * j.start:2 * j.stop].bitcast(FP4X4), lhsT_scale=sc[:, j],
+                                        rhs=codes["q"][:, b].bitcast(FP8X4), rhs_scale=planes["q"][:, b], start=True, stop=True)
+                else:
+                    j = slice(a * 512 + t * P, a * 512 + (t + 1) * P)
+                    for k in range(G):
+                        if kind == "r1":
+                            lhs, lhs_scale, rhs = m1[:, k, j], sc[4 + 4 * k:P, j], "r0"
+                        else:
+                            lhs, lhs_scale, rhs = codes["e"][:, k, j], planes["e"][:, k, j], "r1"
+                        nc.tensor.matmul_mx(out=bank[:], lhsT=lhs.bitcast(FP8X4), lhsT_scale=lhs_scale,
+                                            rhs=codes[rhs][:, k, cols(b)].bitcast(FP8X4), rhs_scale=planes[rhs][:, k, cols(b)],
+                                            start=(k == 0), stop=(k == G - 1))
+
+        def evac(kind, a, b, engine):
+            if kind == "e":
+                dst = stage.tile([P, T, W], BF16, tag="e_rows", name="e_rows", bufs=3, align_bytes=64)
+            elif kind == "r1":
+                dst = stage.tile([P, T, CHUNKS[b]], F32, tag="r1_rows", name="r1_rows", bufs=3, align_bytes=64)
+            else:
+                dst = acc[a, b]
+            rows[kind, a, b] = dst
+            for t in range(T):
+                bank = banks[kind, a, b, t]
+                i = slice(a * T + t, a * T + t + 1)
+                if kind == "e":
+                    nc.scalar.activation(out=dst[:, t], in_=bank[:], func=ACT.Exp, bias=log_u[:, i])
+                elif kind == "r1" and engine == "a":
+                    nc.scalar.activation(out=dst[:, t], in_=bank[:], func=ACT.Copy, scale=w1s[:, i])
+                elif kind == "r1":
+                    nc.vector.tensor_scalar(out=dst[:, t], in0=bank[:], scalar1=w1s[:, i], scalar2=None, op0=ALU.mult)
+                else:
+                    nc.vector.scalar_tensor_tensor(out=dst[:, t], in0=bank[:], scalar=vec["w2"][:, i], in1=dst[:, t], op0=ALU.mult, op1=ALU.add)
+
+        def residual(g, c, engine):
+            for t in range(T):
+                i = slice(g * T + t, g * T + t + 1)
+                if engine == "v":
+                    nc.vector.tensor_scalar(out=acc[g, c][:, t], in0=rows["r1", g, c][:, t], scalar1=b2s[:, i], scalar2=None, op0=ALU.mult)
+                elif engine == "g":
+                    nc.gpsimd.tensor_scalar(out=acc[g, c][:, t], in0=rows["r1", g, c][:, t], scalar1=b2s[:, i], scalar2=0.0, op0=ALU.mult, op1=ALU.add)
+                else:
+                    nc.scalar.activation(out=acc[g, c][:, t], in_=rows["r1", g, c][:, t], func=ACT.Copy, scale=b2s[:, i])
+
+        def interleave(kind, a, b, engine):
+            src = r0_raw[a, b][:] if kind == "r0" else rows[kind, a, b][:]
+            wd = width(kind, b)
+            dst = stage.tile([P, wd, T], BF16, tag="packed", name="packed", bufs=4, align_bytes=64)
+            packed[kind, a, b] = dst
+            cut = {"v": wd, "a": 0, "g": 0, "va": wd * 5 // 8}[engine]
+            for eng, part in (("v", slice(0, cut)), (engine[-1], slice(cut, wd))):
+                if part.start == part.stop:
+                    continue
+                o = dst[:, part].rearrange("p (c i) t -> p c t i", i=4)
+                s = src[:, :, part].rearrange("p t (c i) -> p c t i", i=4)
+                if eng == "v":
+                    nc.vector.tensor_copy(out=o, in_=s)
+                elif eng == "g":
+                    nc.gpsimd.tensor_scalar(out=o, in0=s, scalar1=1.0, scalar2=0.0, op0=ALU.mult, op1=ALU.add)
+                else:
+                    nc.scalar.copy(out=o, in_=s)
+
+        def quantize(kind, a, b):
+            nc.vector.quantize_mx(out=codes[kind][:, a, cols(b, kind)].bitcast(FP8X4), scales=planes[kind][:, a, cols(b, kind)],
+                                  in_=packed[kind, a, b][:].rearrange("p w t -> p (w t)"))
+
+        def store_y(h, c):
+            nc.sync.dma_start(out=out_0[h * 512:(h + 1) * 512, cols(c)].rearrange("(p t) w -> p t w", t=T), in_=acc[h, c][:])
+
+        def store_words(h, c):
+            nc.sync.dma_start(out=out_1[h, :, cols(c), :].rearrange("p m t -> p (m t)").bitcast(I32), in_=codes["y"][:, h, cols(c)].bitcast(I32))
+
+        def store_scales(h, queue):
+            for q in range(4):
+                eng = nc.sync if queue == "s" else nc.scalar
+                eng.dma_start(out=out_2[h, 4 * q:4 * q + 4, :].bitcast(I32), in_=planes["y"][32 * q:32 * q + 4, h].bitcast(I32))
+
+        steps = {"setup": setup, "lv": load_small, "lk": load_k2, "lks": load_k2_scales, "lms": load_m1_scales, "lr": load_r0, "lq": load_q, "lm": load_m1,
+                 "log": log_of_u, "sumlog": sum_logs, "signs": signed_scales, "pk2": permute_k2, "psc": permute_scales, "pm1": permute_m1,
+                 "tq": transpose_q, "eq": evac_q, "mm": matmuls, "ev": evac, "res": residual, "il": interleave, "qz": quantize,
+                 "sy": store_y, "sw": store_words, "ss": store_scales}
+        for entry in ORDER:
+            step, args = steps[entry[0]], entry[1:]
+            step(*args)

@@ -20,32 +20,33 @@ P = 128
 T = 4
 G = N // (P * T)
 W = 512
+GBUFS = 1
 CHUNKS = [512, 512, 512]
 STARTS = [sum(CHUNKS[:c]) for c in range(len(CHUNKS))]
 
 ORDER = [
-    ("setup",), ("lv", "u"), ("lq", 1), ("log",), ("sumlog",), ("lms",),
-    ("lr", 1, 0), ("tq", 1), ("eq", 1, "a"), ("lq", 0), ("tq", 0), ("il", "r0", 1, 0, "v"),
-    ("lks",), ("lk",), ("psc",), ("qz", "q", 1, 0), ("eq", 0, "a"), ("pk2", 0),
-    ("pk2", 1), ("lr", 1, 2), ("qz", "q", 0, 0), ("lr", 1, 1), ("qz", "r0", 1, 0), ("il", "r0", 1, 1, "v"),
-    ("lm", 0), ("lv", "b2"), ("il", "r0", 1, 2, "a"), ("qz", "r0", 1, 2), ("lr", 0, 2), ("il", "r0", 0, 2, "v"),
-    ("qz", "r0", 1, 1), ("mm", "e", 0, 1), ("ev", "e", 0, 1, "a"), ("mm", "e", 1, 1), ("qz", "r0", 0, 2), ("ev", "e", 1, 1, "a"),
-    ("lr", 0, 1), ("lr", 0, 0), ("mm", "e", 0, 0), ("il", "e", 0, 1, "va"), ("mm", "e", 1, 0), ("il", "r0", 0, 0, "v"),
-    ("lm", 1), ("pm1", 1), ("lv", "w2"), ("pm1", 0), ("ev", "e", 0, 0, "a"), ("qz", "e", 0, 1),
-    ("ev", "e", 1, 0, "a"), ("lv", "w1"), ("qz", "r0", 0, 0), ("mm", "r1", 1, 0), ("signs",), ("il", "e", 1, 1, "v"),
-    ("il", "r0", 0, 1, "va"), ("qz", "e", 1, 1), ("il", "e", 0, 0, "v"), ("ev", "r1", 1, 0, "a"), ("il", "e", 1, 0, "v"), ("res", 1, 0, "v"),
-    ("mm", "r1", 0, 0), ("qz", "r0", 0, 1), ("mm", "r1", 0, 1), ("ev", "r1", 0, 0, "a"), ("il", "r1", 1, 0, "va"), ("qz", "e", 1, 0),
-    ("res", 0, 0, "v"), ("ev", "r1", 0, 1, "a"), ("mm", "r1", 1, 1), ("ev", "r1", 1, 1, "a"), ("il", "r1", 0, 0, "v"), ("res", 0, 1, "v"),
-    ("qz", "r1", 1, 0), ("mm", "r1", 0, 2), ("ev", "r1", 0, 2, "a"), ("qz", "e", 0, 0), ("qz", "r1", 0, 0), ("mm", "y", 0, 0),
-    ("il", "r1", 1, 1, "v"), ("ev", "y", 0, 0, "v"), ("qz", "r1", 1, 1), ("il", "r1", 0, 1, "a"), ("il", "y", 0, 0, "v"), ("mm", "y", 1, 0),
-    ("qz", "r1", 0, 1), ("qz", "y", 0, 0), ("mm", "r1", 1, 2), ("il", "r1", 0, 2, "a"), ("ev", "y", 1, 0, "v"), ("qz", "r1", 0, 2),
-    ("ev", "r1", 1, 2, "a"), ("res", 1, 1, "a"), ("il", "r1", 1, 2, "a"), ("sy", 0, 0), ("res", 0, 2, "a"), ("sy", 1, 0),
-    ("mm", "y", 1, 1), ("ev", "y", 1, 1, "v"), ("sw", 0, 0), ("mm", "y", 0, 1), ("ev", "y", 0, 1, "v"), ("qz", "r1", 1, 2),
-    ("mm", "y", 0, 2), ("res", 1, 2, "v"), ("mm", "y", 1, 2), ("sy", 1, 1), ("sy", 0, 1), ("ev", "y", 0, 2, "v"),
-    ("sy", 0, 2), ("ev", "y", 1, 2, "v"), ("il", "y", 0, 1, "va"), ("il", "y", 1, 0, "a"), ("il", "y", 0, 2, "a"), ("sy", 1, 2),
-    ("qz", "y", 0, 2), ("qz", "y", 0, 1), ("qz", "y", 1, 0), ("ss", 0, "s"), ("sw", 0, 2), ("il", "y", 1, 1, "a"),
-    ("sw", 0, 1), ("il", "y", 1, 2, "va"), ("qz", "y", 1, 1), ("sw", 1, 0), ("sw", 1, 1), ("qz", "y", 1, 2),
-    ("ss", 1, "a"), ("sw", 1, 2),
+    ("setup",), ("lq", 0), ("lv", "u", "a"), ("log",), ("lk",), ("tq", 0),
+    ("pk2", 0), ("sumlog",), ("lv", "w1", "a"), ("pk2", 1), ("lks",), ("lr", 0, 0),
+    ("il", "r0", 0, 0, "va"), ("qz", "r0", 0, 0), ("lq", 1), ("lms",), ("psc",), ("tq", 1),
+    ("lr", 1, 0), ("eq", 0, "a"), ("qz", "q", 0, 0), ("lm", 0), ("lm", 1), ("il", "r0", 1, 0, "va"),
+    ("lv", "b2", "s"), ("eq", 1, "a"), ("mm", "e", 0, 0), ("lr", 0, 2), ("lr", 0, 1), ("pm1", 0),
+    ("lr", 1, 2), ("ev", "e", 0, 0, "a"), ("qz", "r0", 1, 0), ("mm", "e", 1, 0), ("qz", "q", 1, 0), ("pm1", 1),
+    ("mm", "r1", 1, 0), ("signs",), ("il", "r0", 0, 2, "v"), ("ev", "r1", 1, 0, "v"), ("ev", "e", 1, 0, "a"), ("il", "r0", 1, 2, "v"),
+    ("il", "e", 0, 0, "gv"), ("mm", "e", 0, 1), ("qz", "r0", 1, 2), ("ev", "e", 0, 1, "a"), ("lv", "w2", "s"), ("mm", "r1", 0, 0),
+    ("qz", "r0", 0, 2), ("il", "e", 1, 0, "v"), ("il", "r1", 1, 0, "v"), ("qz", "e", 1, 0), ("qz", "e", 0, 0), ("mm", "r1", 1, 2),
+    ("ev", "r1", 0, 0, "a"), ("lr", 1, 1), ("res", 1, 0, "a"), ("il", "r0", 1, 1, "v"), ("mm", "e", 1, 1), ("il", "r1", 0, 0, "a"),
+    ("ev", "r1", 1, 2, "v"), ("il", "e", 0, 1, "gv"), ("il", "r0", 0, 1, "v"), ("qz", "r1", 0, 0), ("qz", "r1", 1, 0), ("res", 1, 2, "v"),
+    ("res", 0, 0, "a"), ("ev", "e", 1, 1, "a"), ("mm", "r1", 0, 2), ("qz", "r0", 0, 1), ("qz", "r0", 1, 1), ("qz", "e", 0, 1),
+    ("il", "r1", 1, 2, "v"), ("mm", "y", 0, 0), ("ev", "y", 0, 0, "v"), ("ev", "r1", 0, 2, "a"), ("il", "r1", 0, 2, "gv"), ("sy", 0, 0),
+    ("mm", "r1", 0, 1), ("il", "e", 1, 1, "a"), ("mm", "r1", 1, 1), ("ev", "r1", 0, 1, "a"), ("ev", "r1", 1, 1, "a"), ("qz", "e", 1, 1),
+    ("qz", "r1", 0, 2), ("mm", "y", 1, 0), ("qz", "r1", 1, 2), ("il", "r1", 0, 1, "ga"), ("ev", "y", 1, 0, "v"), ("sy", 1, 0),
+    ("mm", "y", 1, 2), ("mm", "y", 0, 2), ("ev", "y", 1, 2, "v"), ("il", "r1", 1, 1, "Ga"), ("res", 0, 2, "a"), ("qz", "r1", 0, 1),
+    ("sy", 1, 2), ("qz", "r1", 1, 1), ("mm", "y", 0, 1), ("ev", "y", 0, 2, "v"), ("sy", 0, 2), ("res", 0, 1, "a"),
+    ("ev", "y", 0, 1, "v"), ("sy", 0, 1), ("mm", "y", 1, 1), ("il", "y", 1, 0, "g"), ("res", 1, 1, "a"), ("il", "y", 0, 0, "Ga"),
+    ("ev", "y", 1, 1, "v"), ("il", "y", 0, 2, "G"), ("qz", "y", 0, 2), ("sy", 1, 1), ("il", "y", 0, 1, "a"), ("qz", "y", 0, 0),
+    ("sw", 0, 2), ("sw", 0, 0), ("qz", "y", 0, 1), ("ss", 0, "s"), ("sw", 0, 1), ("il", "y", 1, 2, "a"),
+    ("il", "y", 1, 1, "va"), ("qz", "y", 1, 2), ("sw", 1, 2), ("qz", "y", 1, 1), ("qz", "y", 1, 0), ("sw", 1, 1),
+    ("ss", 1, "s"), ("sw", 1, 0),
 ]
 
 
@@ -118,8 +119,8 @@ def tile_rollout_two_layers_k4_kernel(tc, q2, k2_words, k2_scales, m1t_words, m1
             nc.vector.memset(sc_raw[:].bitcast(I32), 0)
             make_identity(nc, ident[:])
 
-        def load_small(name):
-            load_vec(name, {"u": u, "w1": w1, "w2": w2, "b2": b2}[name], nc.sync if name == "u" else nc.gpsimd)
+        def load_small(name, queue):
+            load_vec(name, {"u": u, "w1": w1, "w2": w2, "b2": b2}[name], {"s": nc.sync, "a": nc.scalar, "g": nc.gpsimd}[queue])
 
         def load_k2():
             nc.sync.dma_start(out=k2_raw[:].bitcast(I32), in_=k2_words[0].bitcast(I32))
@@ -230,10 +231,14 @@ def tile_rollout_two_layers_k4_kernel(tc, q2, k2_words, k2_scales, m1t_words, m1
         def interleave(kind, a, b, engine):
             src = r0_raw[a, b][:] if kind == "r0" else rows[kind, a, b][:]
             wd = width(kind, b)
-            dst = stage.tile([P, wd, T], BF16, tag="packed", name="packed", bufs=4, align_bytes=64)
+            if "g" in engine:
+                dst = stage.tile([P, wd, T], BF16, tag="gpacked", name="gpacked", bufs=GBUFS, align_bytes=64)
+            else:
+                dst = stage.tile([P, wd, T], BF16, tag="packed", name="packed", bufs=4, align_bytes=64)
             packed[kind, a, b] = dst
-            cut = {"v": wd, "a": 0, "g": 0, "va": wd * 5 // 8}[engine]
-            for eng, part in (("v", slice(0, cut)), (engine[-1], slice(cut, wd))):
+            engine = engine.replace("G", "g")
+            cut = {"v": wd, "a": wd, "g": wd, "va": wd * 5 // 8, "ga": wd * 3 // 4, "gv": wd * 3 // 4}[engine]
+            for eng, part in ((engine[0], slice(0, cut)), (engine[-1], slice(cut, wd))):
                 if part.start == part.stop:
                     continue
                 o = dst[:, part].rearrange("p (c i) t -> p c t i", i=4)

from contextlib import ExitStack

import concourse.mybir as mybir
from concourse.masks import make_identity

N, D, C = 1024, 512, 1536
FLOPS = 2 * N * N * D + 2 * 2 * N * N * C

F32 = mybir.dt.float32
BF16 = mybir.dt.bfloat16
I32 = mybir.dt.int32
U32 = mybir.dt.uint32
U8 = mybir.dt.uint8
FP8X4 = mybir.dt.float8_e4m3fn_x4
FP4X4 = mybir.dt.float4_e2m1fn_x4
ALU = mybir.AluOpType
ACT = mybir.ActivationFunctionType

P = 128
T = 4
G = N // (P * T)
W = 512
GBUFS = 1
CHUNKS = [512, 512, 512]
STARTS = [sum(CHUNKS[:c]) for c in range(len(CHUNKS))]

ORDER = [
    ("setup",), ("lq", 0), ("lv", "u", "a"), ("log",), ("lk",), ("tq", 0),
    ("pk2", 0), ("sumlog",), ("lv", "w1", "a"), ("pk2", 1), ("lks",), ("lr", 0, 0),
    ("il", "r0", 0, 0, "va"), ("qz", "r0", 0, 0), ("lq", 1), ("lms",), ("psc",), ("tq", 1),
    ("lr", 1, 0), ("eq", 0, "a"), ("qz", "q", 0, 0), ("lm", 0), ("lm", 1), ("il", "r0", 1, 0, "va"),
    ("lv", "b2", "s"), ("eq", 1, "a"), ("mm", "e", 0, 0), ("lr", 0, 2), ("lr", 0, 1), ("pm1", 0),
    ("lr", 1, 2), ("ev", "e", 0, 0, "a"), ("qz", "r0", 1, 0), ("mm", "e", 1, 0), ("qz", "q", 1, 0), ("pm1", 1),
    ("mm", "r1", 1, 0), ("signs",), ("il", "r0", 0, 2, "v"), ("ev", "r1", 1, 0, "v"), ("ev", "e", 1, 0, "a"), ("il", "r0", 1, 2, "v"),
    ("il", "e", 0, 0, "gv"), ("mm", "e", 0, 1), ("qz", "r0", 1, 2), ("ev", "e", 0, 1, "a"), ("lv", "w2", "s"), ("mm", "r1", 0, 0),
    ("qz", "r0", 0, 2), ("il", "e", 1, 0, "v"), ("il", "r1", 1, 0, "v"), ("qz", "e", 1, 0), ("qz", "e", 0, 0), ("mm", "r1", 1, 2),
    ("ev", "r1", 0, 0, "a"), ("lr", 1, 1), ("res", 1, 0, "a"), ("il", "r0", 1, 1, "v"), ("mm", "e", 1, 1), ("il", "r1", 0, 0, "a"),
    ("ev", "r1", 1, 2, "v"), ("il", "e", 0, 1, "gv"), ("il", "r0", 0, 1, "v"), ("qz", "r1", 0, 0), ("qz", "r1", 1, 0), ("res", 1, 2, "v"),
    ("res", 0, 0, "a"), ("ev", "e", 1, 1, "a"), ("mm", "r1", 0, 2), ("qz", "r0", 0, 1), ("qz", "r0", 1, 1), ("qz", "e", 0, 1),
    ("il", "r1", 1, 2, "v"), ("mm", "y", 0, 0), ("ev", "y", 0, 0, "v"), ("ev", "r1", 0, 2, "a"), ("il", "r1", 0, 2, "gv"), ("sy", 0, 0),
    ("mm", "r1", 0, 1), ("il", "e", 1, 1, "a"), ("mm", "r1", 1, 1), ("ev", "r1", 0, 1, "a"), ("ev", "r1", 1, 1, "a"), ("qz", "e", 1, 1),
    ("qz", "r1", 0, 2), ("mm", "y", 1, 0), ("qz", "r1", 1, 2), ("il", "r1", 0, 1, "ga"), ("ev", "y", 1, 0, "v"), ("sy", 1, 0),
    ("mm", "y", 1, 2), ("mm", "y", 0, 2), ("ev", "y", 1, 2, "v"), ("il", "r1", 1, 1, "Ga"), ("res", 0, 2, "a"), ("qz", "r1", 0, 1),
    ("sy", 1, 2), ("qz", "r1", 1, 1), ("mm", "y", 0, 1), ("ev", "y", 0, 2, "v"), ("sy", 0, 2), ("res", 0, 1, "a"),
    ("ev", "y", 0, 1, "v"), ("sy", 0, 1), ("mm", "y", 1, 1), ("il", "y", 1, 0, "g"), ("res", 1, 1, "a"), ("il", "y", 0, 0, "Ga"),
    ("ev", "y", 1, 1, "v"), ("il", "y", 0, 2, "G"), ("qz", "y", 0, 2), ("sy", 1, 1), ("il", "y", 0, 1, "a"), ("qz", "y", 0, 0),
    ("sw", 0, 2), ("sw", 0, 0), ("qz", "y", 0, 1), ("ss", 0, "s"), ("sw", 0, 1), ("il", "y", 1, 2, "a"),
    ("il", "y", 1, 1, "va"), ("qz", "y", 1, 2), ("sw", 1, 2), ("qz", "y", 1, 1), ("qz", "y", 1, 0), ("sw", 1, 1),
    ("ss", 1, "s"), ("sw", 1, 0),
]


def tile_rollout_two_layers_k4_kernel(tc, q2, k2_words, k2_scales, m1t_words, m1t_scales, r0, u, w1, w2, b2, out_0, out_1, out_2):
    nc = tc.nc
    with ExitStack() as ctx:
        keep = ctx.enter_context(tc.tile_pool(name="keep", bufs=1))
        stage = ctx.enter_context(tc.tile_pool(name="stage", bufs=2))
        psum = ctx.enter_context(tc.psum_pool(name="psum", bufs=8))
        ctx.enter_context(tc.manual_schedule())

        def kept(name, shape, dtype):
            return keep.tile(shape, dtype, name=name, align_bytes=64)

        vec = {}
        for name in ("u", "w1", "w2", "b2"):
            vec[name] = kept("vec_" + name, [P, G * T], BF16)
        ident = kept("ident", [P, P], F32)
        sc_raw = kept("sc_raw", [P, N], U8)
        sc = kept("sc", [P, N], U8)
        k2_raw = kept("k2_raw", [P, 2 * N], U8)
        k2 = kept("k2", [P, 2 * N], U8)
        m1_raw = kept("m1_raw", [P, G, N], I32)
        m1 = kept("m1", [P, G, N], I32)
        q_raw = kept("q_raw", [P, G, T, D], BF16)
        r0_raw = {}
        acc = {}
        for g in range(G):
            for c, width in enumerate(CHUNKS):
                r0_raw[g, c] = kept("r0_raw%d_%d" % (g, c), [P, T, width], BF16)
                acc[g, c] = kept("acc%d_%d" % (g, c), [P, T, width], F32)
        codes = {}
        planes = {}
        for name, cols in (("q", [G, W]), ("r0", [G, C]), ("e", [G, N]), ("r1", [G, C]), ("y", [G, C])):
            codes[name] = kept("codes_" + name, [P] + cols, U32)
            planes[name] = kept("plane_" + name, [P] + cols, U8)
        mag = kept("mag", [P, G * T], F32)
        parts = kept("parts", [P, 4, G * T], F32)
        logs = kept("logs", [P, 4, G * T], F32)
        log_u = kept("log_u", [P, G * T], F32)
        sign2 = kept("sign2", [P, G * T], F32)
        w1s = kept("w1s", [P, G * T], F32)
        b2s = kept("b2s", [P, G * T], F32)
        warm = kept("warm", [P, 2], F32)
        banks = {}
        rows = {}
        packed = {}

        def cols(c, kind="r0"):
            if kind in ("q", "e"):
                return slice(c * W, (c + 1) * W)
            return slice(STARTS[c], STARTS[c] + CHUNKS[c])

        def width(kind, c):
            return W if kind in ("q", "e") else CHUNKS[c]

        def load_vec(name, src, queue):
            queue.dma_start(out=vec[name][:].rearrange("p (g t) -> p g t", t=T), in_=src.rearrange("(g p t) -> p g t", g=G, t=T))

        def load_r0(g, c):
            nc.sync.dma_start(out=r0_raw[g, c][:], in_=r0[g * 512:(g + 1) * 512, cols(c)].rearrange("(p t) w -> p t w", t=T))

        def load_q(h):
            nc.sync.dma_start(out=q_raw[:, h], in_=q2[h * 512:(h + 1) * 512, :].rearrange("(m t) d -> m t d", t=T))

        def load_m1(k):
            nc.sync.dma_start(out=m1_raw[:, k], in_=m1t_words[k].rearrange("p n t -> p (n t)").bitcast(I32))

        def setup():
            nc.vector.memset(sc_raw[:].bitcast(I32), 0)
            make_identity(nc, ident[:])

        def load_small(name, queue):
            load_vec(name, {"u": u, "w1": w1, "w2": w2, "b2": b2}[name], {"s": nc.sync, "a": nc.scalar, "g": nc.gpsimd}[queue])

        def load_k2():
            nc.sync.dma_start(out=k2_raw[:].bitcast(I32), in_=k2_words[0].bitcast(I32))

        def load_k2_scales():
            for q in range(4):
                nc.sync.dma_start(out=sc_raw[32 * q:32 * q + 4, :].bitcast(I32), in_=k2_scales[0, 4 * q:4 * q + 4, :].bitcast(I32))

        def load_m1_scales():
            for q in range(4):
                nc.sync.dma_start(out=sc_raw[32 * q + 4:32 * q + 12, :].bitcast(I32), in_=m1t_scales[:, 4 * q:4 * q + 4, :].bitcast(I32))

        def log_of_u():
            nc.vector.scalar_tensor_tensor(out=mag[:], in0=vec["u"][:], scalar=-1.0, in1=vec["u"][:], op0=ALU.mult, op1=ALU.max)
            nc.vector.tensor_scalar(out=sign2[:], in0=vec["u"][:], scalar1=0.0, scalar2=2.0, op0=ALU.is_ge, op1=ALU.mult)
            nc.vector.tensor_scalar(out=parts[:, 0], in0=mag[:], scalar1=2.0 ** -63, scalar2=2.0 ** 64, op0=ALU.max, op1=ALU.min)
            nc.vector.tensor_scalar(out=parts[:, 1], in0=mag[:], scalar1=2.0 ** 64, scalar2=2.0 ** -64, op0=ALU.max, op1=ALU.mult)
            nc.vector.tensor_scalar(out=parts[:, 2], in0=mag[:], scalar1=2.0 ** -126, scalar2=2.0 ** -63, op0=ALU.max, op1=ALU.min)
            nc.vector.tensor_scalar(out=logs[:, 3], in0=mag[:], scalar1=2.0 ** -126, scalar2=-(2.0 ** 100), op0=ALU.is_lt, op1=ALU.mult)
            nc.scalar.activation(out=logs[:, 0:2], in_=parts[:, 0:2], func=ACT.Ln)
            nc.scalar.activation(out=logs[:, 2], in_=parts[:, 2], func=ACT.Ln, scale=2.0 ** 63)
            nc.scalar.activation(out=warm[:, 0:1], in_=logs[:, 2, 0:1], func=ACT.Exp)

        def sum_logs():
            nc.vector.tensor_reduce(out=log_u[:], in_=logs[:].rearrange("p k j -> p j k"), axis=mybir.AxisListType.X, op=ALU.add)

        def signed_scales():
            nc.vector.scalar_tensor_tensor(out=w1s[:], in0=sign2[:], scalar=1.0, in1=vec["w1"][:], op0=ALU.subtract, op1=ALU.mult)
            nc.vector.scalar_tensor_tensor(out=b2s[:], in0=sign2[:], scalar=1.0, in1=vec["b2"][:], op0=ALU.subtract, op1=ALU.mult)

        def permute_k2(g):
            s = slice(g * 1024, (g + 1) * 1024)
            nc.vector.tensor_copy(out=k2[:, s].rearrange("p (t m b) -> p t m b", t=T, b=2), in_=k2_raw[:, s].rearrange("p (m t b) -> p t m b", t=T, b=2))

        def permute_scales():
            nc.vector.tensor_copy(out=sc[:].rearrange("p (g t m) -> p g t m", g=G, t=T), in_=sc_raw[:].rearrange("p (g m t) -> p g t m", g=G, t=T))

        def permute_m1(k):
            nc.vector.tensor_copy(out=m1[:, k].rearrange("p (g t m) -> p g t m", g=G, t=T), in_=m1_raw[:, k].rearrange("p (g m t) -> p g t m", g=G, t=T))

        def transpose_q(h):
            words = q_raw[:, h].bitcast(F32)
            for half in range(2):
                bank = psum.tile([P, 2, 2, P], F32, tag="bank", name="bank")
                banks["q", h, half] = bank
                for s in range(2):
                    for e in range(2):
                        nc.tensor.transpose(bank[:, s, e, :], words[:, 2 * half + s, e:256:2], ident[:])

        def evac_q(h, engine):
            dst = stage.tile([P, W, T], BF16, tag="packed", name="packed", bufs=4, align_bytes=64)
            packed["q", h, 0] = dst
            words = dst[:].rearrange("p w t -> p (w t)").bitcast(F32)
            for half in range(2):
                copy = nc.scalar.copy if engine == "a" else nc.vector.tensor_copy
                copy(out=words[:, half * 512:(half + 1) * 512].rearrange("p (s m e) -> p s m e", s=2, e=2), in_=banks["q", h, half][:].rearrange("p s e m -> p s m e"))

        def matmuls(kind, a, b):
            for t in range(T):
                whole = psum.tile([P, W], F32, tag="bank", name="bank")
                bank = whole[:, 0:width(kind, b)]
                banks[kind, a, b, t] = bank
                if kind == "e":
                    j = slice(a * 512 + t * P, a * 512 + (t + 1) * P)
                    nc.tensor.matmul_mx(out=bank[:], lhsT=k2[:, 2 * j.start:2 * j.stop].bitcast(FP4X4), lhsT_scale=sc[:, j],
                                        rhs=codes["q"][:, b].bitcast(FP8X4), rhs_scale=planes["q"][:, b], start=True, stop=True)
                else:
                    j = slice(a * 512 + t * P, a * 512 + (t + 1) * P)
                    for k in range(G):
                        if kind == "r1":
                            lhs, lhs_scale, rhs = m1[:, k, j], sc[4 + 4 * k:P, j], "r0"
                        else:
                            lhs, lhs_scale, rhs = codes["e"][:, k, j], planes["e"][:, k, j], "r1"
                        nc.tensor.matmul_mx(out=bank[:], lhsT=lhs.bitcast(FP8X4), lhsT_scale=lhs_scale,
                                            rhs=codes[rhs][:, k, cols(b)].bitcast(FP8X4), rhs_scale=planes[rhs][:, k, cols(b)],
                                            start=(k == 0), stop=(k == G - 1))

        def evac(kind, a, b, engine):
            if kind == "e":
                dst = stage.tile([P, T, W], BF16, tag="e_rows", name="e_rows", bufs=3, align_bytes=64)
            elif kind == "r1":
                dst = stage.tile([P, T, CHUNKS[b]], F32, tag="r1_rows", name="r1_rows", bufs=3, align_bytes=64)
            else:
                dst = acc[a, b]
            rows[kind, a, b] = dst
            for t in range(T):
                bank = banks[kind, a, b, t]
                i = slice(a * T + t, a * T + t + 1)
                if kind == "e":
                    nc.scalar.activation(out=dst[:, t], in_=bank[:], func=ACT.Exp, bias=log_u[:, i])
                elif kind == "r1" and engine == "a":
                    nc.scalar.activation(out=dst[:, t], in_=bank[:], func=ACT.Copy, scale=w1s[:, i])
                elif kind == "r1":
                    nc.vector.tensor_scalar(out=dst[:, t], in0=bank[:], scalar1=w1s[:, i], scalar2=None, op0=ALU.mult)
                else:
                    nc.vector.scalar_tensor_tensor(out=dst[:, t], in0=bank[:], scalar=vec["w2"][:, i], in1=dst[:, t], op0=ALU.mult, op1=ALU.add)

        def residual(g, c, engine):
            for t in range(T):
                i = slice(g * T + t, g * T + t + 1)
                if engine == "v":
                    nc.vector.tensor_scalar(out=acc[g, c][:, t], in0=rows["r1", g, c][:, t], scalar1=b2s[:, i], scalar2=None, op0=ALU.mult)
                elif engine == "g":
                    nc.gpsimd.tensor_scalar(out=acc[g, c][:, t], in0=rows["r1", g, c][:, t], scalar1=b2s[:, i], scalar2=0.0, op0=ALU.mult, op1=ALU.add)
                else:
                    nc.scalar.activation(out=acc[g, c][:, t], in_=rows["r1", g, c][:, t], func=ACT.Copy, scale=b2s[:, i])

        def interleave(kind, a, b, engine):
            src = r0_raw[a, b][:] if kind == "r0" else rows[kind, a, b][:]
            wd = width(kind, b)
            if "g" in engine:
                dst = stage.tile([P, wd, T], BF16, tag="gpacked", name="gpacked", bufs=GBUFS, align_bytes=64)
            else:
                dst = stage.tile([P, wd, T], BF16, tag="packed", name="packed", bufs=4, align_bytes=64)
            packed[kind, a, b] = dst
            engine = engine.replace("G", "g")
            cut = {"v": wd, "a": wd, "g": wd, "va": wd * 5 // 8, "ga": wd * 3 // 4, "gv": wd * 3 // 4}[engine]
            for eng, part in ((engine[0], slice(0, cut)), (engine[-1], slice(cut, wd))):
                if part.start == part.stop:
                    continue
                o = dst[:, part].rearrange("p (c i) t -> p c t i", i=4)
                s = src[:, :, part].rearrange("p t (c i) -> p c t i", i=4)
                if eng == "v":
                    nc.vector.tensor_copy(out=o, in_=s)
                elif eng == "g":
                    nc.gpsimd.tensor_scalar(out=o, in0=s, scalar1=1.0, scalar2=0.0, op0=ALU.mult, op1=ALU.add)
                else:
                    nc.scalar.copy(out=o, in_=s)

        def quantize(kind, a, b):
            nc.vector.quantize_mx(out=codes[kind][:, a, cols(b, kind)].bitcast(FP8X4), scales=planes[kind][:, a, cols(b, kind)],
                                  in_=packed[kind, a, b][:].rearrange("p w t -> p (w t)"))

        def store_y(h, c):
            nc.sync.dma_start(out=out_0[h * 512:(h + 1) * 512, cols(c)].rearrange("(p t) w -> p t w", t=T), in_=acc[h, c][:])

        def store_words(h, c):
            nc.sync.dma_start(out=out_1[h, :, cols(c), :].rearrange("p m t -> p (m t)").bitcast(I32), in_=codes["y"][:, h, cols(c)].bitcast(I32))

        def store_scales(h, queue):
            for q in range(4):
                eng = nc.sync if queue == "s" else nc.scalar
                eng.dma_start(out=out_2[h, 4 * q:4 * q + 4, :].bitcast(I32), in_=planes["y"][32 * q:32 * q + 4, h].bitcast(I32))

        steps = {"setup": setup, "lv": load_small, "lk": load_k2, "lks": load_k2_scales, "lms": load_m1_scales, "lr": load_r0, "lq": load_q, "lm": load_m1,
                 "log": log_of_u, "sumlog": sum_logs, "signs": signed_scales, "pk2": permute_k2, "psc": permute_scales, "pm1": permute_m1,
                 "tq": transpose_q, "eq": evac_q, "mm": matmuls, "ev": evac, "res": residual, "il": interleave, "qz": quantize,
                 "sy": store_y, "sw": store_words, "ss": store_scales}
        for entry in ORDER:
            step, args = steps[entry[0]], entry[1:]
            step(*args)
